import numpy as np
import ml_dtypes


def mxq(x, axis, fmt="e4m3"):
    dtype, down = {"e4m3": (ml_dtypes.float8_e4m3fn, 7), "e5m2": (ml_dtypes.float8_e5m2, 14)}[fmt]
    v = np.moveaxis(np.asarray(x, np.float32).astype(ml_dtypes.bfloat16).astype(np.float64), axis, -1)
    blocks = v.reshape(v.shape[:-1] + (-1, 32))
    amax = np.abs(blocks).max(-1, keepdims=True)
    byte = np.maximum(np.where(amax > 0, np.frexp(amax)[1] - 1 + 127, 0) - down, 1)
    scale = np.exp2(byte - 127.0)
    codes = (blocks / scale).astype(np.float32).astype(dtype).astype(np.float64)
    return np.moveaxis((codes * scale).reshape(v.shape), -1, axis)


WIDE = False


def mx_kscale(k):
    if not WIDE:
        return np.ones(k)
    levels = np.array([10, -10, 5, -5, 0])
    if k % 512:
        return np.exp2(np.random.permutation(np.resize(levels, k // 32))).repeat(32)
    a = np.empty((k // 512, 16))
    for p in range(k // 512):
        a[p, :8] = np.random.permutation(np.resize(levels, 8))
        for g in range(8):
            far = levels[np.abs(levels - a[p, g]) >= 10]
            a[p, g + 8] = far[np.random.randint(len(far))]
    return np.exp2(a.ravel()).repeat(32)


def f64(x):
    return np.asarray(x).astype(np.float64)


def striped(idx):
    return np.tile(idx.reshape(-1, 16).T, (8, 1)).astype(np.uint16)


def unstriped(offs):
    return offs[:16].T.reshape(-1).astype(np.int64)


def pack_weight(w):
    k, n = w.shape
    w = f64(np.asarray(w, np.float32).astype(ml_dtypes.bfloat16)).reshape(k // 32, 32, n)
    amax = np.abs(w).max(1)
    byte = np.clip(np.where(amax > 0, np.frexp(amax)[1] - 1 + 127 - 7, 1), 1, 254)
    scaled = (w * np.exp2(127.0 - byte)[:, None, :]).reshape(k, n).astype(np.float32)
    words = np.ascontiguousarray(scaled.reshape(k // 512, 128, 4, n).transpose(0, 1, 3, 2)).astype(ml_dtypes.float8_e4m3fn).view(np.uint8)
    return words, np.ascontiguousarray(byte.astype(np.uint8).reshape(k // 512, 16, n))


def unpack_weight(words, scales):
    g, p, n, _ = words.shape
    vals = np.ascontiguousarray(words).view(ml_dtypes.float8_e4m3fn).astype(np.float64) * np.repeat(np.exp2(scales.astype(np.float64) - 127.0), 8, axis=1)[..., None]
    return vals.transpose(0, 1, 3, 2).reshape(g * 512, n)


def relu(v):
    return np.maximum(v, 0.0)


K, T, S, V, H, N = 1024, 1024, 512, 256, 512, 128


def setup_inputs():
    n = np.random.standard_normal
    s = mx_kscale(K)[:, None]
    u = mx_kscale(H)
    packed_xT = pack_weight(n((K, T)) * s)
    return {
        "x_words": packed_xT[0],
        "x_scales": packed_xT[1],
        "w1": (n((K, H)) / np.sqrt(K) / s * u).astype(np.float32),
        "w2": (n((H, N)) / np.sqrt(H) / u[:, None]).astype(np.float32),
        "offs": striped(np.random.permutation(T)[:S]),
    }


def reference(x_words, x_scales, w1, w2, offs):
    xq = unpack_weight(x_words, x_scales)[:, unstriped(offs)]
    h = relu(mxq(f64(w1), 0, "e4m3").T @ xq)
    z = np.abs(h[:, :V] - h[:, V:2 * V])
    return mxq(f64(w2), 0, "e4m3").T @ mxq(z, 0, "e4m3")

@@ -1,0 +1,142 @@
+from contextlib import ExitStack
+
+import concourse.mybir as mybir
+
+K, T, S, V, H, N = 1024, 1024, 512, 256, 512, 128
+FLOPS = 2 * K * H * S + 2 * H * N * V
+
+F32 = mybir.dt.float32
+BF16 = mybir.dt.bfloat16
+I32 = mybir.dt.int32
+U32 = mybir.dt.uint32
+U16 = mybir.dt.uint16
+U8 = mybir.dt.uint8
+FP8X4 = mybir.dt.float8_e4m3fn_x4
+ALU = mybir.AluOpType
+ACT = mybir.ActivationFunctionType
+
+P = 128
+PACK = 4
+K_PASS = P * PACK
+PASSES = K // K_PASS
+QUADS = 4
+VECTOR_M = 84
+HALF = V // 2
+
+
+def tile_picked_siam_abs_p_kernel(tc, x_words, x_scales, w1, w2, offs, out):
+    nc = tc.nc
+    with ExitStack() as ctx:
+        keep = ctx.enter_context(tc.tile_pool(name="keep", bufs=1))
+        psum = ctx.enter_context(tc.psum_pool(name="psum", bufs=1))
+
+        offsets = keep.tile([P, S // 16], U16, name="offsets")
+        nc.sync.dma_start(offsets[:], offs)
+
+        scale_table = keep.tile([P, T], U8, name="scale_table", align_bytes=64)
+        nc.vector.memset(scale_table[:].bitcast(I32), 0)
+        for q in range(QUADS):
+            nc.scalar.dma_start(
+                out=scale_table[32 * q : 32 * q + 4 * PASSES, :].bitcast(I32),
+                in_=x_scales[:, 4 * q : 4 * q + 4, :].bitcast(I32),
+            )
+
+        word_tables = []
+        w1_raw = []
+        for z in range(PASSES):
+            table = keep.tile([P, T], I32, name=f"word_table{z}", align_bytes=64)
+            nc.sync.dma_start(out=table[:], in_=x_words[z].rearrange("p c r -> p (c r)").bitcast(I32))
+            word_tables.append(table)
+            raw = keep.tile([P, PACK, H], F32, name=f"w1_raw{z}", align_bytes=64)
+            nc.sync.dma_start(out=raw[:], in_=w1[z * K_PASS : (z + 1) * K_PASS, :].rearrange("(p j) c -> p j c", j=PACK))
+            w1_raw.append(raw)
+        w2_raw = keep.tile([P, PACK, N], F32, name="w2_raw", align_bytes=64)
+        nc.sync.dma_start(out=w2_raw[:], in_=w2.rearrange("(p j) c -> p j c", j=PACK))
+
+        x_scale = keep.tile([P, S], U8, name="x_scale", align_bytes=64)
+        nc.vector.tensor_copy(x_scale[:], scale_table[:].indirect(offsets[:]))
+
+        hidden = [psum.tile([P, S], F32, name=f"hidden{t}") for t in range(PACK)]
+        for z in range(PASSES):
+            x_code = keep.tile([P, S], U32, name=f"x_code{z}", align_bytes=64)
+            nc.vector.tensor_copy(x_code[:], word_tables[z][:].bitcast(U32).indirect(offsets[:]))
+
+            grouped = keep.tile([P, PACK, P, PACK], BF16, name=f"w1_grouped{z}", align_bytes=64)
+            src = w1_raw[z][:].rearrange("p j (m t) -> p m j t", t=PACK)
+            dst = grouped[:].rearrange("p t m j -> p m j t")
+            nc.vector.tensor_copy(out=dst[:, :VECTOR_M], in_=src[:, :VECTOR_M])
+            nc.scalar.copy(out=dst[:, VECTOR_M:], in_=src[:, VECTOR_M:])
+
+            for t in range(PACK):
+                w1_code = keep.tile([P, P], U32, name=f"w1_code{z}_{t}", align_bytes=64)
+                w1_scale = keep.tile([P, P], U8, name=f"w1_scale{z}_{t}", align_bytes=64)
+                nc.vector.quantize_mx(
+                    out=w1_code[:].bitcast(FP8X4),
+                    scales=w1_scale[:],
+                    in_=grouped[:, t].rearrange("p m j -> p (m j)"),
+                )
+                nc.tensor.matmul_mx(
+                    out=hidden[t][:],
+                    lhsT=w1_code[:].bitcast(FP8X4),
+                    lhsT_scale=w1_scale[:],
+                    rhs=x_code[:].bitcast(FP8X4),
+                    rhs_scale=x_scale[4 * z : P, :],
+                    start=(z == 0),
+                    stop=(z == PASSES - 1),
+                )
+
+        w2_grouped = keep.tile([P, N, PACK], BF16, name="w2_grouped", align_bytes=64)
+        nc.scalar.copy(
+            out=w2_grouped[:].rearrange("p (c i) j -> p c j i", i=4),
+            in_=w2_raw[:].rearrange("p j (c i) -> p c j i", i=4),
+        )
+        w2_code = keep.tile([P, N], U32, name="w2_code", align_bytes=64)
+        w2_scale = keep.tile([P, N], U8, name="w2_scale", align_bytes=64)
+        nc.vector.quantize_mx(
+            out=w2_code[:].bitcast(FP8X4), scales=w2_scale[:], in_=w2_grouped[:].rearrange("p c j -> p (c j)")
+        )
+
+        diff = keep.tile([P, PACK, V], F32, name="diff", align_bytes=64)
+        for t in range(PACK):
+            second = keep.tile([P, V], F32, name=f"second{t}", align_bytes=64)
+            nc.scalar.activation(second[:], hidden[t][:, V:], ACT.Relu)
+            nc.vector.scalar_tensor_tensor(
+                out=diff[:, t, :], in0=hidden[t][:, :V], scalar=0.0, in1=second[:], op0=ALU.max, op1=ALU.subtract
+            )
+
+        for h in range(2):
+            pairs = slice(h * HALF, (h + 1) * HALF)
+            z_grouped = keep.tile([P, HALF, PACK], BF16, name=f"z_grouped{h}", align_bytes=64)
+            if h == 0:
+                view = diff[:, :, pairs].rearrange("p t v -> p v t")
+                nc.vector.scalar_tensor_tensor(
+                    out=z_grouped[:], in0=view, scalar=-1.0, in1=view, op0=ALU.mult, op1=ALU.max
+                )
+            else:
+                nc.scalar.activation(
+                    z_grouped[:].rearrange("p (c i) t -> p c t i", i=4),
+                    diff[:, :, pairs].rearrange("p t (c i) -> p c t i", i=4),
+                    ACT.Abs,
+                )
+            z_code = keep.tile([P, HALF], U32, name=f"z_code{h}", align_bytes=64)
+            z_scale = keep.tile([P, HALF], U8, name=f"z_scale{h}", align_bytes=64)
+            nc.vector.quantize_mx(
+                out=z_code[:].bitcast(FP8X4), scales=z_scale[:], in_=z_grouped[:].rearrange("p v t -> p (v t)")
+            )
+            projected = psum.tile([P, HALF], F32, name=f"projected{h}")
+            nc.tensor.matmul_mx(
+                out=projected[:],
+                lhsT=w2_code[:].bitcast(FP8X4),
+                lhsT_scale=w2_scale[:],
+                rhs=z_code[:].bitcast(FP8X4),
+                rhs_scale=z_scale[:],
+                start=True,
+                stop=True,
+            )
+            result = keep.tile([P, HALF], F32, name=f"result{h}", align_bytes=64)
+            if h == 0:
+                nc.scalar.copy(out=result[:], in_=projected[:])
+                nc.scalar.dma_start(out=out[:, pairs], in_=result[:])
+            else:
+                nc.vector.tensor_copy(out=result[:], in_=projected[:])
+                nc.sync.dma_start(out=out[:, pairs], in_=result[:])

@@ -20,8 +20,8 @@ PACK = 4
 K_PASS = P * PACK
 PASSES = K // K_PASS
 QUADS = 4
-VECTOR_M = 84
 HALF = V // 2
+VECTOR_ABS = 64
 
 
 def tile_picked_siam_abs_p_kernel(tc, x_words, x_scales, w1, w2, offs, out):
@@ -30,100 +30,129 @@ def tile_picked_siam_abs_p_kernel(tc, x_words, x_scales, w1, w2, offs, out):
         keep = ctx.enter_context(tc.tile_pool(name="keep", bufs=1))
         psum = ctx.enter_context(tc.psum_pool(name="psum", bufs=1))
 
-        offsets = keep.tile([P, S // 16], U16, name="offsets")
-        nc.sync.dma_start(offsets[:], offs)
-
         scale_table = keep.tile([P, T], U8, name="scale_table", align_bytes=64)
         nc.vector.memset(scale_table[:].bitcast(I32), 0)
+        warm = keep.tile([P, 16], F32, name="warm", align_bytes=64)
+        nc.gpsimd.memset(warm[:, 0:1], 0.0)
+        nc.scalar.activation(warm[:, 8:9], warm[:, 0:1], ACT.Abs)
+
+        def load_words(z):
+            table = keep.tile([P, T], I32, name=f"word_table{z}", align_bytes=64)
+            nc.sync.dma_start(out=table[:], in_=x_words[z].rearrange("p c r -> p (c r)").bitcast(I32))
+            return table
+
+        def load_rows(name, rows):
+            raw = keep.tile([P, PACK, rows.shape[1]], F32, name=name, align_bytes=64)
+            nc.sync.dma_start(out=raw[:], in_=rows.rearrange("(p j) c -> p j c", j=PACK))
+            return raw
+
+        word_table0 = load_words(0)
+        offsets = keep.tile([P, S // 16], U16, name="offsets")
+        nc.sync.dma_start(offsets[:], offs)
         for q in range(QUADS):
-            nc.scalar.dma_start(
+            queue = nc.gpsimd if q < 0 else nc.sync
+            queue.dma_start(
                 out=scale_table[32 * q : 32 * q + 4 * PASSES, :].bitcast(I32),
                 in_=x_scales[:, 4 * q : 4 * q + 4, :].bitcast(I32),
             )
+        w1_raw = [load_rows(f"w1_raw{z}", w1[z * K_PASS : (z + 1) * K_PASS, :]) for z in range(PASSES)]
+        word_table1 = load_words(1)
+        w2_raw = load_rows("w2_raw", w2)
 
-        word_tables = []
-        w1_raw = []
-        for z in range(PASSES):
-            table = keep.tile([P, T], I32, name=f"word_table{z}", align_bytes=64)
-            nc.sync.dma_start(out=table[:], in_=x_words[z].rearrange("p c r -> p (c r)").bitcast(I32))
-            word_tables.append(table)
-            raw = keep.tile([P, PACK, H], F32, name=f"w1_raw{z}", align_bytes=64)
-            nc.sync.dma_start(out=raw[:], in_=w1[z * K_PASS : (z + 1) * K_PASS, :].rearrange("(p j) c -> p j c", j=PACK))
-            w1_raw.append(raw)
-        w2_raw = keep.tile([P, PACK, N], F32, name="w2_raw", align_bytes=64)
-        nc.sync.dma_start(out=w2_raw[:], in_=w2.rearrange("(p j) c -> p j c", j=PACK))
-
+        hidden = [[psum.tile([P, V], F32, name=f"hidden{h}_{t}") for t in range(PACK)] for h in range(2)]
         x_scale = keep.tile([P, S], U8, name="x_scale", align_bytes=64)
-        nc.vector.tensor_copy(x_scale[:], scale_table[:].indirect(offsets[:]))
+        x_code = [keep.tile([P, S], U32, name=f"x_code{z}", align_bytes=64) for z in range(PASSES)]
 
-        hidden = [psum.tile([P, S], F32, name=f"hidden{t}") for t in range(PACK)]
-        for z in range(PASSES):
-            x_code = keep.tile([P, S], U32, name=f"x_code{z}", align_bytes=64)
-            nc.vector.tensor_copy(x_code[:], word_tables[z][:].bitcast(U32).indirect(offsets[:]))
+        def interleave(z):
+            grouped = []
+            for u, copy in enumerate((nc.vector.tensor_copy, nc.scalar.copy)):
+                tile = keep.tile([P, 2, P, PACK], BF16, name=f"w1_grouped{z}_{u}", align_bytes=64)
+                src = w1_raw[z][:].rearrange("p j (m t) -> p m j t", t=PACK)[:, :, :, 2 * u : 2 * u + 2]
+                copy(out=tile[:].rearrange("p t m j -> p m j t"), in_=src)
+                grouped.append(tile)
+            return grouped
 
-            grouped = keep.tile([P, PACK, P, PACK], BF16, name=f"w1_grouped{z}", align_bytes=64)
-            src = w1_raw[z][:].rearrange("p j (m t) -> p m j t", t=PACK)
-            dst = grouped[:].rearrange("p t m j -> p m j t")
-            nc.vector.tensor_copy(out=dst[:, :VECTOR_M], in_=src[:, :VECTOR_M])
-            nc.scalar.copy(out=dst[:, VECTOR_M:], in_=src[:, VECTOR_M:])
+        def quantize(name, grouped, width):
+            code = keep.tile([P, width], U32, name=name + "_code", align_bytes=64)
+            scale = keep.tile([P, width], U8, name=name + "_scale", align_bytes=64)
+            nc.vector.quantize_mx(out=code[:].bitcast(FP8X4), scales=scale[:], in_=grouped)
+            return code, scale
 
-            for t in range(PACK):
-                w1_code = keep.tile([P, P], U32, name=f"w1_code{z}_{t}", align_bytes=64)
-                w1_scale = keep.tile([P, P], U8, name=f"w1_scale{z}_{t}", align_bytes=64)
-                nc.vector.quantize_mx(
-                    out=w1_code[:].bitcast(FP8X4),
-                    scales=w1_scale[:],
-                    in_=grouped[:, t].rearrange("p m j -> p (m j)"),
+        def gather(dst, table, runs):
+            for place, entry, count in runs:
+                nc.vector.tensor_copy(
+                    dst[:, place * HALF : (place + count) * HALF],
+                    table.indirect(offsets[:, entry * HALF // 16 : (entry + count) * HALF // 16]),
                 )
+
+        def products(z, h, u, code, scale):
+            cols = slice((1 - h) * V, (2 - h) * V)
+            for s in range(2):
                 nc.tensor.matmul_mx(
-                    out=hidden[t][:],
-                    lhsT=w1_code[:].bitcast(FP8X4),
-                    lhsT_scale=w1_scale[:],
-                    rhs=x_code[:].bitcast(FP8X4),
-                    rhs_scale=x_scale[4 * z : P, :],
+                    out=hidden[h][2 * u + s][:],
+                    lhsT=code[:, s * P : (s + 1) * P].bitcast(FP8X4),
+                    lhsT_scale=scale[:, s * P : (s + 1) * P],
+                    rhs=x_code[z][:, cols].bitcast(FP8X4),
+                    rhs_scale=x_scale[4 * z : P, cols],
                     start=(z == 0),
                     stop=(z == PASSES - 1),
                 )
+
+        three = ((1, 1, 2), (0, 3, 1), (3, 0, 1))
+        gather(x_code[0], word_table0[:].bitcast(U32), three)
+        gather(x_scale, scale_table[:], three)
+        grouped = interleave(0)
+        for u in range(2):
+            code, scale = quantize(f"w1_0_{u}", grouped[u][:].rearrange("p t m j -> p (t m j)"), 2 * P)
+            for h in range(2):
+                products(0, h, u, code, scale)
+
+        grouped = interleave(1)
+        coded = []
+        for u in range(2):
+            coded.append(quantize(f"w1_1_{u}", grouped[u][:].rearrange("p t m j -> p (t m j)"), 2 * P))
+            gather(x_code[1], word_table1[:].bitcast(U32), ((2 - 2 * u, 2 + u, 1), (3 - 2 * u, u, 1)))
+        for h in range(2):
+            for u in range(2):
+                products(1, h, u, *coded[u])
 
         w2_grouped = keep.tile([P, N, PACK], BF16, name="w2_grouped", align_bytes=64)
         nc.scalar.copy(
             out=w2_grouped[:].rearrange("p (c i) j -> p c j i", i=4),
             in_=w2_raw[:].rearrange("p j (c i) -> p c j i", i=4),
         )
-        w2_code = keep.tile([P, N], U32, name="w2_code", align_bytes=64)
-        w2_scale = keep.tile([P, N], U8, name="w2_scale", align_bytes=64)
-        nc.vector.quantize_mx(
-            out=w2_code[:].bitcast(FP8X4), scales=w2_scale[:], in_=w2_grouped[:].rearrange("p c j -> p (c j)")
-        )
+        w2_code, w2_scale = quantize("w2", w2_grouped[:].rearrange("p c j -> p (c j)"), N)
 
-        diff = keep.tile([P, PACK, V], F32, name="diff", align_bytes=64)
-        for t in range(PACK):
-            second = keep.tile([P, V], F32, name=f"second{t}", align_bytes=64)
-            nc.scalar.activation(second[:], hidden[t][:, V:], ACT.Relu)
-            nc.vector.scalar_tensor_tensor(
-                out=diff[:, t, :], in0=hidden[t][:, :V], scalar=0.0, in1=second[:], op0=ALU.max, op1=ALU.subtract
+        diff = [keep.tile([P, PACK, HALF], F32, name=f"diff{h}", align_bytes=64) for h in range(2)]
+        for h in range(2):
+            for t in range(PACK):
+                second_relu = keep.tile([P, HALF], F32, name=f"second_relu{h}_{t}", align_bytes=64)
+                nc.scalar.activation(second_relu[:], hidden[h][t][:, :HALF], ACT.Relu)
+                nc.vector.scalar_tensor_tensor(
+                    out=diff[h][:, t, :],
+                    in0=hidden[h][t][:, HALF:],
+                    scalar=0.0,
+                    in1=second_relu[:],
+                    op0=ALU.max,
+                    op1=ALU.subtract,
+                )
+
+        z_grouped = [keep.tile([P, HALF, PACK], BF16, name=f"z_grouped{h}", align_bytes=64) for h in range(2)]
+        for h, count in enumerate((HALF, HALF - VECTOR_ABS)):
+            nc.scalar.activation(
+                z_grouped[h][:, :count, :].rearrange("p (c i) t -> p c t i", i=4),
+                diff[h][:, :, :count].rearrange("p t (c i) -> p c t i", i=4),
+                ACT.Abs,
             )
+        view = diff[1][:, :, HALF - VECTOR_ABS :].rearrange("p t v -> p v t")
+        nc.vector.scalar_tensor_tensor(
+            out=z_grouped[1][:, HALF - VECTOR_ABS :, :], in0=view, scalar=-1.0, in1=view, op0=ALU.mult, op1=ALU.max
+        )
 
         for h in range(2):
             pairs = slice(h * HALF, (h + 1) * HALF)
-            z_grouped = keep.tile([P, HALF, PACK], BF16, name=f"z_grouped{h}", align_bytes=64)
-            if h == 0:
-                view = diff[:, :, pairs].rearrange("p t v -> p v t")
-                nc.vector.scalar_tensor_tensor(
-                    out=z_grouped[:], in0=view, scalar=-1.0, in1=view, op0=ALU.mult, op1=ALU.max
-                )
-            else:
-                nc.scalar.activation(
-                    z_grouped[:].rearrange("p (c i) t -> p c t i", i=4),
-                    diff[:, :, pairs].rearrange("p t (c i) -> p c t i", i=4),
-                    ACT.Abs,
-                )
-            z_code = keep.tile([P, HALF], U32, name=f"z_code{h}", align_bytes=64)
-            z_scale = keep.tile([P, HALF], U8, name=f"z_scale{h}", align_bytes=64)
-            nc.vector.quantize_mx(
-                out=z_code[:].bitcast(FP8X4), scales=z_scale[:], in_=z_grouped[:].rearrange("p v t -> p (v t)")
-            )
-            projected = psum.tile([P, HALF], F32, name=f"projected{h}")
+            z_code, z_scale = quantize(f"z{h}", z_grouped[h][:].rearrange("p v t -> p (v t)"), HALF)
+            projected = psum.tile([P, HALF], F32, name=f"projected{h}", tag=f"hidden0_{h}")
             nc.tensor.matmul_mx(
                 out=projected[:],
                 lhsT=w2_code[:].bitcast(FP8X4),

@@ -20,8 +20,10 @@ PACK = 4
 K_PASS = P * PACK
 PASSES = K // K_PASS
 QUADS = 4
-HALF = V // 2
-VECTOR_ABS = 64
+CHUNK = 128
+CHUNKS = V // CHUNK
+FIRST, SECOND = 0, 1
+VECTOR_COLS = 32
 
 
 def tile_picked_siam_abs_p_kernel(tc, x_words, x_scales, w1, w2, offs, out):
@@ -50,8 +52,7 @@ def tile_picked_siam_abs_p_kernel(tc, x_words, x_scales, w1, w2, offs, out):
         offsets = keep.tile([P, S // 16], U16, name="offsets")
         nc.sync.dma_start(offsets[:], offs)
         for q in range(QUADS):
-            queue = nc.gpsimd if q < 0 else nc.sync
-            queue.dma_start(
+            nc.sync.dma_start(
                 out=scale_table[32 * q : 32 * q + 4 * PASSES, :].bitcast(I32),
                 in_=x_scales[:, 4 * q : 4 * q + 4, :].bitcast(I32),
             )
@@ -59,17 +60,21 @@ def tile_picked_siam_abs_p_kernel(tc, x_words, x_scales, w1, w2, offs, out):
         word_table1 = load_words(1)
         w2_raw = load_rows("w2_raw", w2)
 
-        hidden = [[psum.tile([P, V], F32, name=f"hidden{h}_{t}") for t in range(PACK)] for h in range(2)]
+        banks = [(c, side) for c in range(CHUNKS) for side in (SECOND, FIRST)]
+        hidden = {key: psum.tile([P, PACK, CHUNK], F32, name=f"hidden{key[0]}_{key[1]}") for key in banks}
         x_scale = keep.tile([P, S], U8, name="x_scale", align_bytes=64)
         x_code = [keep.tile([P, S], U32, name=f"x_code{z}", align_bytes=64) for z in range(PASSES)]
 
+        def entries(c, side):
+            return slice(side * V + c * CHUNK, side * V + (c + 1) * CHUNK)
+
         def interleave(z):
-            grouped = []
-            for u, copy in enumerate((nc.vector.tensor_copy, nc.scalar.copy)):
-                tile = keep.tile([P, 2, P, PACK], BF16, name=f"w1_grouped{z}_{u}", align_bytes=64)
-                src = w1_raw[z][:].rearrange("p j (m t) -> p m j t", t=PACK)[:, :, :, 2 * u : 2 * u + 2]
-                copy(out=tile[:].rearrange("p t m j -> p m j t"), in_=src)
-                grouped.append(tile)
+            src = w1_raw[z][:].rearrange("p j (m t) -> p m j t", t=PACK)
+            grouped = [keep.tile([P, 2, P, PACK], BF16, name=f"w1_grouped{z}_{u}", align_bytes=64) for u in range(2)]
+            dst = [tile[:].rearrange("p t m j -> p m j t") for tile in grouped]
+            nc.scalar.copy(out=dst[1][:, VECTOR_COLS:], in_=src[:, VECTOR_COLS:, :, 2:4])
+            nc.vector.tensor_copy(out=dst[0], in_=src[:, :, :, 0:2])
+            nc.vector.tensor_copy(out=dst[1][:, :VECTOR_COLS], in_=src[:, :VECTOR_COLS, :, 2:4])
             return grouped
 
         def quantize(name, grouped, width):
@@ -78,43 +83,41 @@ def tile_picked_siam_abs_p_kernel(tc, x_words, x_scales, w1, w2, offs, out):
             nc.vector.quantize_mx(out=code[:].bitcast(FP8X4), scales=scale[:], in_=grouped)
             return code, scale
 
-        def gather(dst, table, runs):
-            for place, entry, count in runs:
-                nc.vector.tensor_copy(
-                    dst[:, place * HALF : (place + count) * HALF],
-                    table.indirect(offsets[:, entry * HALF // 16 : (entry + count) * HALF // 16]),
-                )
+        def quantize_w1(z):
+            grouped = interleave(z)
+            return [
+                quantize(f"w1_{z}_{u}", grouped[u][:].rearrange("p t m j -> p (t m j)"), 2 * P) for u in range(2)
+            ]
 
-        def products(z, h, u, code, scale):
-            cols = slice((1 - h) * V, (2 - h) * V)
-            for s in range(2):
-                nc.tensor.matmul_mx(
-                    out=hidden[h][2 * u + s][:],
-                    lhsT=code[:, s * P : (s + 1) * P].bitcast(FP8X4),
-                    lhsT_scale=scale[:, s * P : (s + 1) * P],
-                    rhs=x_code[z][:, cols].bitcast(FP8X4),
-                    rhs_scale=x_scale[4 * z : P, cols],
-                    start=(z == 0),
-                    stop=(z == PASSES - 1),
-                )
+        def product(z, key, t, coded):
+            code, scale = coded[t // 2]
+            m = slice((t % 2) * P, (t % 2 + 1) * P)
+            cols = entries(*key)
+            nc.tensor.matmul_mx(
+                out=hidden[key][:, t, :],
+                lhsT=code[:, m].bitcast(FP8X4),
+                lhsT_scale=scale[:, m],
+                rhs=x_code[z][:, cols].bitcast(FP8X4),
+                rhs_scale=x_scale[4 * z : P, cols],
+                start=(z == 0 and t == 0),
+                stop=(z == PASSES - 1 and t == PACK - 1),
+            )
 
-        three = ((1, 1, 2), (0, 3, 1), (3, 0, 1))
-        gather(x_code[0], word_table0[:].bitcast(U32), three)
-        gather(x_scale, scale_table[:], three)
-        grouped = interleave(0)
-        for u in range(2):
-            code, scale = quantize(f"w1_0_{u}", grouped[u][:].rearrange("p t m j -> p (t m j)"), 2 * P)
-            for h in range(2):
-                products(0, h, u, code, scale)
+        nc.vector.tensor_copy(x_code[0][:], word_table0[:].bitcast(U32).indirect(offsets[:]))
+        nc.vector.tensor_copy(x_scale[:], scale_table[:].indirect(offsets[:]))
+        coded = quantize_w1(0)
+        for t in range(PACK):
+            for key in banks:
+                product(0, key, t, coded)
 
-        grouped = interleave(1)
-        coded = []
-        for u in range(2):
-            coded.append(quantize(f"w1_1_{u}", grouped[u][:].rearrange("p t m j -> p (t m j)"), 2 * P))
-            gather(x_code[1], word_table1[:].bitcast(U32), ((2 - 2 * u, 2 + u, 1), (3 - 2 * u, u, 1)))
-        for h in range(2):
-            for u in range(2):
-                products(1, h, u, *coded[u])
+        coded = quantize_w1(1)
+        for key in banks:
+            cols = entries(*key)
+            nc.vector.tensor_copy(
+                x_code[1][:, cols], word_table1[:].bitcast(U32).indirect(offsets[:, cols.start // 16 : cols.stop // 16])
+            )
+            for t in range(PACK):
+                product(1, key, t, coded)
 
         w2_grouped = keep.tile([P, N, PACK], BF16, name="w2_grouped", align_bytes=64)
         nc.scalar.copy(
@@ -123,36 +126,44 @@ def tile_picked_siam_abs_p_kernel(tc, x_words, x_scales, w1, w2, offs, out):
         )
         w2_code, w2_scale = quantize("w2", w2_grouped[:].rearrange("p c j -> p (c j)"), N)
 
-        diff = [keep.tile([P, PACK, HALF], F32, name=f"diff{h}", align_bytes=64) for h in range(2)]
-        for h in range(2):
-            for t in range(PACK):
-                second_relu = keep.tile([P, HALF], F32, name=f"second_relu{h}_{t}", align_bytes=64)
-                nc.scalar.activation(second_relu[:], hidden[h][t][:, :HALF], ACT.Relu)
+        PIECE = CHUNK // 2
+        diff = []
+        for c in range(CHUNKS):
+            second_relu = keep.tile([P, CHUNK, PACK], F32, name=f"second_relu{c}", align_bytes=64)
+            signed = keep.tile([P, CHUNK, PACK], BF16, name=f"diff{c}", align_bytes=64)
+            for lo in range(0, CHUNK, PIECE):
+                part = slice(lo, lo + PIECE)
+                nc.scalar.activation(
+                    second_relu[:, part, :], hidden[c, SECOND][:, :, part].rearrange("p t v -> p v t"), ACT.Relu
+                )
                 nc.vector.scalar_tensor_tensor(
-                    out=diff[h][:, t, :],
-                    in0=hidden[h][t][:, HALF:],
+                    out=signed[:, part, :],
+                    in0=hidden[c, FIRST][:, :, part].rearrange("p t v -> p v t"),
                     scalar=0.0,
-                    in1=second_relu[:],
+                    in1=second_relu[:, part, :],
                     op0=ALU.max,
                     op1=ALU.subtract,
                 )
+            diff.append(signed[:].rearrange("p v t -> p (v t)"))
 
-        z_grouped = [keep.tile([P, HALF, PACK], BF16, name=f"z_grouped{h}", align_bytes=64) for h in range(2)]
-        for h, count in enumerate((HALF, HALF - VECTOR_ABS)):
-            nc.scalar.activation(
-                z_grouped[h][:, :count, :].rearrange("p (c i) t -> p c t i", i=4),
-                diff[h][:, :, :count].rearrange("p t (c i) -> p c t i", i=4),
-                ACT.Abs,
-            )
-        view = diff[1][:, :, HALF - VECTOR_ABS :].rearrange("p t v -> p v t")
-        nc.vector.scalar_tensor_tensor(
-            out=z_grouped[1][:, HALF - VECTOR_ABS :, :], in0=view, scalar=-1.0, in1=view, op0=ALU.mult, op1=ALU.max
-        )
-
-        for h in range(2):
-            pairs = slice(h * HALF, (h + 1) * HALF)
-            z_code, z_scale = quantize(f"z{h}", z_grouped[h][:].rearrange("p v t -> p (v t)"), HALF)
-            projected = psum.tile([P, HALF], F32, name=f"projected{h}", tag=f"hidden0_{h}")
+        for c in range(CHUNKS):
+            pairs = slice(c * CHUNK, (c + 1) * CHUNK)
+            z_grouped = keep.tile([P, CHUNK * PACK], BF16, name=f"z_grouped{c}", align_bytes=64)
+            if c == 0:
+                nc.scalar.activation(z_grouped[:], diff[c], ACT.Abs)
+            else:
+                for lo in range(0, CHUNK * PACK, PIECE * PACK):
+                    part = slice(lo, lo + PIECE * PACK)
+                    nc.vector.scalar_tensor_tensor(
+                        out=z_grouped[:, part],
+                        in0=diff[c][:, part],
+                        scalar=-1.0,
+                        in1=diff[c][:, part],
+                        op0=ALU.mult,
+                        op1=ALU.max,
+                    )
+            z_code, z_scale = quantize(f"z{c}", z_grouped[:], CHUNK)
+            projected = psum.tile([P, CHUNK], F32, name=f"projected{c}")
             nc.tensor.matmul_mx(
                 out=projected[:],
                 lhsT=w2_code[:].bitcast(FP8X4),
@@ -162,8 +173,8 @@ def tile_picked_siam_abs_p_kernel(tc, x_words, x_scales, w1, w2, offs, out):
                 start=True,
                 stop=True,
             )
-            result = keep.tile([P, HALF], F32, name=f"result{h}", align_bytes=64)
-            if h == 0:
+            result = keep.tile([P, CHUNK], F32, name=f"result{c}", align_bytes=64)
+            if c == 0:
                 nc.scalar.copy(out=result[:], in_=projected[:])
                 nc.scalar.dma_start(out=out[:, pairs], in_=result[:])
             else:

@@ -22,7 +22,9 @@ PASSES = K // K_PASS
 QUADS = 4
 CHUNK = 128
 CHUNKS = V // CHUNK
+PIECE = CHUNK // 2
 FIRST, SECOND = 0, 1
+VECTOR_ABS = 32
 VECTOR_COLS = 32
 
 
@@ -32,6 +34,7 @@ def tile_picked_siam_abs_p_kernel(tc, x_words, x_scales, w1, w2, offs, out):
         keep = ctx.enter_context(tc.tile_pool(name="keep", bufs=1))
         psum = ctx.enter_context(tc.psum_pool(name="psum", bufs=1))
 
+        offsets = keep.tile([P, S // 16], U16, name="offsets")
         scale_table = keep.tile([P, T], U8, name="scale_table", align_bytes=64)
         nc.vector.memset(scale_table[:].bitcast(I32), 0)
         warm = keep.tile([P, 16], F32, name="warm", align_bytes=64)
@@ -49,32 +52,37 @@ def tile_picked_siam_abs_p_kernel(tc, x_words, x_scales, w1, w2, offs, out):
             return raw
 
         word_table0 = load_words(0)
-        offsets = keep.tile([P, S // 16], U16, name="offsets")
         nc.sync.dma_start(offsets[:], offs)
         for q in range(QUADS):
             nc.sync.dma_start(
                 out=scale_table[32 * q : 32 * q + 4 * PASSES, :].bitcast(I32),
                 in_=x_scales[:, 4 * q : 4 * q + 4, :].bitcast(I32),
             )
-        w1_raw = [load_rows(f"w1_raw{z}", w1[z * K_PASS : (z + 1) * K_PASS, :]) for z in range(PASSES)]
+        def load_row_pair(z, half):
+            raw = keep.tile([P, 2, H], F32, name=f"w1_raw{z}_{half}", align_bytes=64)
+            rows = w1[z * K_PASS : (z + 1) * K_PASS, :].rearrange("(p j) c -> p j c", j=PACK)
+            nc.sync.dma_start(out=raw[:], in_=rows[:, 2 * half : 2 * half + 2, :])
+            return raw
+
+        w1_raw = [[load_rows("w1_raw0", w1[:K_PASS, :])], [load_row_pair(1, half) for half in range(2)]]
         word_table1 = load_words(1)
         w2_raw = load_rows("w2_raw", w2)
 
         banks = [(c, side) for c in range(CHUNKS) for side in (SECOND, FIRST)]
         hidden = {key: psum.tile([P, PACK, CHUNK], F32, name=f"hidden{key[0]}_{key[1]}") for key in banks}
-        x_scale = keep.tile([P, S], U8, name="x_scale", align_bytes=64)
-        x_code = [keep.tile([P, S], U32, name=f"x_code{z}", align_bytes=64) for z in range(PASSES)]
 
         def entries(c, side):
             return slice(side * V + c * CHUNK, side * V + (c + 1) * CHUNK)
 
-        def interleave(z):
-            src = w1_raw[z][:].rearrange("p j (m t) -> p m j t", t=PACK)
-            grouped = [keep.tile([P, 2, P, PACK], BF16, name=f"w1_grouped{z}_{u}", align_bytes=64) for u in range(2)]
-            dst = [tile[:].rearrange("p t m j -> p m j t") for tile in grouped]
-            nc.scalar.copy(out=dst[1][:, VECTOR_COLS:], in_=src[:, VECTOR_COLS:, :, 2:4])
-            nc.vector.tensor_copy(out=dst[0], in_=src[:, :, :, 0:2])
-            nc.vector.tensor_copy(out=dst[1][:, :VECTOR_COLS], in_=src[:, :VECTOR_COLS, :, 2:4])
+        def interleave(z, tag):
+            grouped = keep.tile([P, PACK * P * PACK], BF16, name=f"w1_grouped{z}", tag=tag, align_bytes=64)
+            rows = PACK // len(w1_raw[z])
+            for i, raw in enumerate(w1_raw[z]):
+                src = raw[:].rearrange("p j (m t) -> p m j t", t=PACK)
+                dst = grouped[:].rearrange("p (t m j) -> p m j t", t=PACK, j=PACK)[:, :, i * rows : (i + 1) * rows, :]
+                nc.scalar.copy(out=dst[:, VECTOR_COLS:, :, 2:4], in_=src[:, VECTOR_COLS:, :, 2:4])
+                nc.vector.tensor_copy(out=dst[:, :, :, 0:2], in_=src[:, :, :, 0:2])
+                nc.vector.tensor_copy(out=dst[:, :VECTOR_COLS, :, 2:4], in_=src[:, :VECTOR_COLS, :, 2:4])
             return grouped
 
         def quantize(name, grouped, width):
@@ -83,41 +91,48 @@ def tile_picked_siam_abs_p_kernel(tc, x_words, x_scales, w1, w2, offs, out):
             nc.vector.quantize_mx(out=code[:].bitcast(FP8X4), scales=scale[:], in_=grouped)
             return code, scale
 
-        def quantize_w1(z):
-            grouped = interleave(z)
-            return [
-                quantize(f"w1_{z}_{u}", grouped[u][:].rearrange("p t m j -> p (t m j)"), 2 * P) for u in range(2)
-            ]
+        def quantize_tiles(z, grouped, lo, hi):
+            code, scale = quantize(f"w1_{z}_{lo}", grouped[:, lo * K_PASS : hi * K_PASS], (hi - lo) * P)
+            return [(code[:, s * P : (s + 1) * P], scale[:, s * P : (s + 1) * P]) for s in range(hi - lo)]
 
-        def product(z, key, t, coded):
-            code, scale = coded[t // 2]
-            m = slice((t % 2) * P, (t % 2 + 1) * P)
+        def product(z, key, t, coded, x_code):
+            code, scale = coded[t]
             cols = entries(*key)
             nc.tensor.matmul_mx(
                 out=hidden[key][:, t, :],
-                lhsT=code[:, m].bitcast(FP8X4),
-                lhsT_scale=scale[:, m],
-                rhs=x_code[z][:, cols].bitcast(FP8X4),
+                lhsT=code.bitcast(FP8X4),
+                lhsT_scale=scale,
+                rhs=x_code[:, cols].bitcast(FP8X4),
                 rhs_scale=x_scale[4 * z : P, cols],
                 start=(z == 0 and t == 0),
                 stop=(z == PASSES - 1 and t == PACK - 1),
             )
 
-        nc.vector.tensor_copy(x_code[0][:], word_table0[:].bitcast(U32).indirect(offsets[:]))
+        x_code0 = keep.tile([P, S], U32, name="x_code0", align_bytes=64)
+        x_scale = keep.tile([P, S], U8, name="x_scale", align_bytes=64)
+        nc.vector.tensor_copy(x_code0[:], word_table0[:].bitcast(U32).indirect(offsets[:]))
         nc.vector.tensor_copy(x_scale[:], scale_table[:].indirect(offsets[:]))
-        coded = quantize_w1(0)
+        grouped0 = interleave(0, "g0")
+        coded = quantize_tiles(0, grouped0, 0, 2) + quantize_tiles(0, grouped0, 2, 4)
         for t in range(PACK):
             for key in banks:
-                product(0, key, t, coded)
+                product(0, key, t, coded, x_code0)
 
-        coded = quantize_w1(1)
-        for key in banks:
+        grouped1 = interleave(1, "g1")
+        x_code1 = keep.tile([P, S], U32, name="x_code1", align_bytes=64)
+
+        def gather_last_pass(key):
             cols = entries(*key)
             nc.vector.tensor_copy(
-                x_code[1][:, cols], word_table1[:].bitcast(U32).indirect(offsets[:, cols.start // 16 : cols.stop // 16])
+                x_code1[:, cols], word_table1[:].bitcast(U32).indirect(offsets[:, cols.start // 16 : cols.stop // 16])
             )
+
+        coded = quantize_tiles(1, grouped1, 0, 2) + quantize_tiles(1, grouped1, 2, 4)
+        for key in banks:
+            gather_last_pass(key)
+        for key in banks:
             for t in range(PACK):
-                product(1, key, t, coded)
+                product(1, key, t, coded, x_code1)
 
         w2_grouped = keep.tile([P, N, PACK], BF16, name="w2_grouped", align_bytes=64)
         nc.scalar.copy(
@@ -126,44 +141,38 @@ def tile_picked_siam_abs_p_kernel(tc, x_words, x_scales, w1, w2, offs, out):
         )
         w2_code, w2_scale = quantize("w2", w2_grouped[:].rearrange("p c j -> p (c j)"), N)
 
-        PIECE = CHUNK // 2
-        diff = []
-        for c in range(CHUNKS):
-            second_relu = keep.tile([P, CHUNK, PACK], F32, name=f"second_relu{c}", align_bytes=64)
-            signed = keep.tile([P, CHUNK, PACK], BF16, name=f"diff{c}", align_bytes=64)
-            for lo in range(0, CHUNK, PIECE):
-                part = slice(lo, lo + PIECE)
-                nc.scalar.activation(
-                    second_relu[:, part, :], hidden[c, SECOND][:, :, part].rearrange("p t v -> p v t"), ACT.Relu
-                )
-                nc.vector.scalar_tensor_tensor(
-                    out=signed[:, part, :],
-                    in0=hidden[c, FIRST][:, :, part].rearrange("p t v -> p v t"),
-                    scalar=0.0,
-                    in1=second_relu[:, part, :],
-                    op0=ALU.max,
-                    op1=ALU.subtract,
-                )
-            diff.append(signed[:].rearrange("p v t -> p (v t)"))
+        diff = keep.tile([P, V * PACK], BF16, name="diff", align_bytes=64)
+        second_relu = keep.tile([P, V * PACK], F32, name="second_relu", align_bytes=64)
+        for lo in range(0, V, PIECE):
+            c, part = lo // CHUNK, slice(lo % CHUNK, lo % CHUNK + PIECE)
+            flat = slice(lo * PACK, (lo + PIECE) * PACK)
+            kept = second_relu[:, flat].rearrange("p (v t) -> p v t", t=PACK)
+            nc.scalar.activation(kept, hidden[c, SECOND][:, :, part].rearrange("p t v -> p v t"), ACT.Relu)
+            nc.vector.scalar_tensor_tensor(
+                out=diff[:, flat].rearrange("p (v t) -> p v t", t=PACK),
+                in0=hidden[c, FIRST][:, :, part].rearrange("p t v -> p v t"),
+                scalar=0.0,
+                in1=kept,
+                op0=ALU.max,
+                op1=ALU.subtract,
+            )
 
-        for c in range(CHUNKS):
-            pairs = slice(c * CHUNK, (c + 1) * CHUNK)
-            z_grouped = keep.tile([P, CHUNK * PACK], BF16, name=f"z_grouped{c}", align_bytes=64)
-            if c == 0:
-                nc.scalar.activation(z_grouped[:], diff[c], ACT.Abs)
-            else:
-                for lo in range(0, CHUNK * PACK, PIECE * PACK):
-                    part = slice(lo, lo + PIECE * PACK)
-                    nc.vector.scalar_tensor_tensor(
-                        out=z_grouped[:, part],
-                        in0=diff[c][:, part],
-                        scalar=-1.0,
-                        in1=diff[c][:, part],
-                        op0=ALU.mult,
-                        op1=ALU.max,
-                    )
-            z_code, z_scale = quantize(f"z{c}", z_grouped[:], CHUNK)
-            projected = psum.tile([P, CHUNK], F32, name=f"projected{c}")
+        z_grouped = keep.tile([P, V * PACK], BF16, name="z_grouped", align_bytes=64)
+
+        def flat(lo, hi):
+            return slice(lo * PACK, hi * PACK)
+
+        def abs_on_vector(lo, hi):
+            signed = diff[:, flat(lo, hi)]
+            nc.vector.scalar_tensor_tensor(
+                out=z_grouped[:, flat(lo, hi)], in0=signed, scalar=-1.0, in1=signed, op0=ALU.mult, op1=ALU.max
+            )
+
+        result = keep.tile([P, V], F32, name="result", align_bytes=64)
+
+        def project(lo, hi, copy):
+            z_code, z_scale = quantize(f"z{lo}", z_grouped[:, flat(lo, hi)], hi - lo)
+            projected = psum.tile([P, hi - lo], F32, name=f"projected{lo}")
             nc.tensor.matmul_mx(
                 out=projected[:],
                 lhsT=w2_code[:].bitcast(FP8X4),
@@ -173,10 +182,15 @@ def tile_picked_siam_abs_p_kernel(tc, x_words, x_scales, w1, w2, offs, out):
                 start=True,
                 stop=True,
             )
-            result = keep.tile([P, CHUNK], F32, name=f"result{c}", align_bytes=64)
-            if c == 0:
-                nc.scalar.copy(out=result[:], in_=projected[:])
-                nc.scalar.dma_start(out=out[:, pairs], in_=result[:])
-            else:
-                nc.vector.tensor_copy(out=result[:], in_=projected[:])
-                nc.sync.dma_start(out=out[:, pairs], in_=result[:])
+            copy(out=result[:, lo:hi], in_=projected[:])
+
+        for lo in range(0, V, PIECE):
+            hi = min(lo + PIECE, V - VECTOR_ABS)
+            if hi > lo:
+                nc.scalar.activation(z_grouped[:, flat(lo, hi)], diff[:, flat(lo, hi)], ACT.Abs)
+        abs_on_vector(V - VECTOR_ABS, V)
+        project(0, CHUNK, nc.scalar.copy)
+        project(CHUNK, V - PIECE, nc.scalar.copy)
+        nc.scalar.dma_start(out=out[:, : V - PIECE], in_=result[:, : V - PIECE])
+        project(V - PIECE, V, nc.vector.tensor_copy)
+        nc.sync.dma_start(out=out[:, V - PIECE :], in_=result[:, V - PIECE :])

@@ -24,7 +24,7 @@ CHUNK = 128
 CHUNKS = V // CHUNK
 PIECE = CHUNK // 2
 FIRST, SECOND = 0, 1
-VECTOR_ABS = 32
+CUTS = (0, 64, 128, 192, 224, 256)
 VECTOR_COLS = 32
 
 
@@ -141,18 +141,19 @@ def tile_picked_siam_abs_p_kernel(tc, x_words, x_scales, w1, w2, offs, out):
         )
         w2_code, w2_scale = quantize("w2", w2_grouped[:].rearrange("p c j -> p (c j)"), N)
 
-        diff = keep.tile([P, V * PACK], BF16, name="diff", align_bytes=64)
-        second_relu = keep.tile([P, V * PACK], F32, name="second_relu", align_bytes=64)
+        def bank_view(side, lo, hi):
+            return hidden[lo // CHUNK, side][:, :, lo % CHUNK : lo % CHUNK + hi - lo].rearrange("p t v -> p v t")
+
+        diff = keep.tile([P, V, PACK], BF16, name="diff", align_bytes=64)
+        second_relu = keep.tile([P, V, PACK], F32, name="second_relu", align_bytes=64)
         for lo in range(0, V, PIECE):
-            c, part = lo // CHUNK, slice(lo % CHUNK, lo % CHUNK + PIECE)
-            flat = slice(lo * PACK, (lo + PIECE) * PACK)
-            kept = second_relu[:, flat].rearrange("p (v t) -> p v t", t=PACK)
-            nc.scalar.activation(kept, hidden[c, SECOND][:, :, part].rearrange("p t v -> p v t"), ACT.Relu)
+            nc.scalar.activation(second_relu[:, lo : lo + PIECE, :], bank_view(SECOND, lo, lo + PIECE), ACT.Relu)
+        for lo, hi in zip(CUTS, CUTS[1:]):
             nc.vector.scalar_tensor_tensor(
-                out=diff[:, flat].rearrange("p (v t) -> p v t", t=PACK),
-                in0=hidden[c, FIRST][:, :, part].rearrange("p t v -> p v t"),
+                out=diff[:, lo:hi, :],
+                in0=bank_view(FIRST, lo, hi),
                 scalar=0.0,
-                in1=kept,
+                in1=second_relu[:, lo:hi, :],
                 op0=ALU.max,
                 op1=ALU.subtract,
             )
@@ -161,12 +162,6 @@ def tile_picked_siam_abs_p_kernel(tc, x_words, x_scales, w1, w2, offs, out):
 
         def flat(lo, hi):
             return slice(lo * PACK, hi * PACK)
-
-        def abs_on_vector(lo, hi):
-            signed = diff[:, flat(lo, hi)]
-            nc.vector.scalar_tensor_tensor(
-                out=z_grouped[:, flat(lo, hi)], in0=signed, scalar=-1.0, in1=signed, op0=ALU.mult, op1=ALU.max
-            )
 
         result = keep.tile([P, V], F32, name="result", align_bytes=64)
 
@@ -184,11 +179,8 @@ def tile_picked_siam_abs_p_kernel(tc, x_words, x_scales, w1, w2, offs, out):
             )
             copy(out=result[:, lo:hi], in_=projected[:])
 
-        for lo in range(0, V, PIECE):
-            hi = min(lo + PIECE, V - VECTOR_ABS)
-            if hi > lo:
-                nc.scalar.activation(z_grouped[:, flat(lo, hi)], diff[:, flat(lo, hi)], ACT.Abs)
-        abs_on_vector(V - VECTOR_ABS, V)
+        for lo, hi in zip(CUTS, CUTS[1:]):
+            nc.scalar.activation(z_grouped[:, flat(lo, hi)], diff[:, lo:hi, :].rearrange("p v t -> p (v t)"), ACT.Abs)
         project(0, CHUNK, nc.scalar.copy)
         project(CHUNK, V - PIECE, nc.scalar.copy)
         nc.scalar.dma_start(out=out[:, : V - PIECE], in_=result[:, : V - PIECE])

@@ -24,6 +24,7 @@ CHUNK = 128
 CHUNKS = V // CHUNK
 PIECE = CHUNK // 2
 FIRST, SECOND = 0, 1
+VECTOR_ABS = slice(160, 192)
 CUTS = (0, 64, 128, 192, 224, 256)
 VECTOR_COLS = 32
 
@@ -179,8 +180,22 @@ def tile_picked_siam_abs_p_kernel(tc, x_words, x_scales, w1, w2, offs, out):
             )
             copy(out=result[:, lo:hi], in_=projected[:])
 
+        def signed(lo, hi):
+            return diff[:, lo:hi, :].rearrange("p v t -> p (v t)")
+
         for lo, hi in zip(CUTS, CUTS[1:]):
-            nc.scalar.activation(z_grouped[:, flat(lo, hi)], diff[:, lo:hi, :].rearrange("p v t -> p (v t)"), ACT.Abs)
+            hi = VECTOR_ABS.start if hi == VECTOR_ABS.stop else hi
+            if hi > lo:
+                nc.scalar.activation(z_grouped[:, flat(lo, hi)], signed(lo, hi), ACT.Abs)
+        lo, hi = VECTOR_ABS.start, VECTOR_ABS.stop
+        nc.vector.scalar_tensor_tensor(
+            out=z_grouped[:, flat(lo, hi)],
+            in0=signed(lo, hi),
+            scalar=-1.0,
+            in1=signed(lo, hi),
+            op0=ALU.mult,
+            op1=ALU.max,
+        )
         project(0, CHUNK, nc.scalar.copy)
         project(CHUNK, V - PIECE, nc.scalar.copy)
         nc.scalar.dma_start(out=out[:, : V - PIECE], in_=result[:, : V - PIECE])

@@ -26,7 +26,7 @@ PIECE = CHUNK // 2
 FIRST, SECOND = 0, 1
 VECTOR_ABS = slice(160, 192)
 CUTS = (0, 64, 128, 192, 224, 256)
-VECTOR_COLS = 32
+VECTOR_COLS = (96, 64)
 
 
 def tile_picked_siam_abs_p_kernel(tc, x_words, x_scales, w1, w2, offs, out):
@@ -81,9 +81,9 @@ def tile_picked_siam_abs_p_kernel(tc, x_words, x_scales, w1, w2, offs, out):
             for i, raw in enumerate(w1_raw[z]):
                 src = raw[:].rearrange("p j (m t) -> p m j t", t=PACK)
                 dst = grouped[:].rearrange("p (t m j) -> p m j t", t=PACK, j=PACK)[:, :, i * rows : (i + 1) * rows, :]
-                nc.scalar.copy(out=dst[:, VECTOR_COLS:, :, 2:4], in_=src[:, VECTOR_COLS:, :, 2:4])
-                nc.vector.tensor_copy(out=dst[:, :, :, 0:2], in_=src[:, :, :, 0:2])
-                nc.vector.tensor_copy(out=dst[:, :VECTOR_COLS, :, 2:4], in_=src[:, :VECTOR_COLS, :, 2:4])
+                for tiles, cols in zip((slice(0, 2), slice(2, 4)), VECTOR_COLS):
+                    nc.vector.tensor_copy(out=dst[:, :cols, :, tiles], in_=src[:, :cols, :, tiles])
+                    nc.scalar.copy(out=dst[:, cols:, :, tiles], in_=src[:, cols:, :, tiles])
             return grouped
 
         def quantize(name, grouped, width):

@@ -36,19 +36,19 @@ def tile_picked_siam_abs_p_kernel(tc, x_words, x_scales, w1, w2, offs, out):
         psum = ctx.enter_context(tc.psum_pool(name="psum", bufs=1))
 
         offsets = keep.tile([P, S // 16], U16, name="offsets")
-        scale_table = keep.tile([P, T], U8, name="scale_table", align_bytes=64)
+        scale_table = keep.tile([P, T], U8, name="scale_table", align_bytes=256)
         nc.vector.memset(scale_table[:].bitcast(I32), 0)
-        warm = keep.tile([P, 16], F32, name="warm", align_bytes=64)
+        warm = keep.tile([P, 16], F32, name="warm", align_bytes=256)
         nc.gpsimd.memset(warm[:, 0:1], 0.0)
         nc.scalar.activation(warm[:, 8:9], warm[:, 0:1], ACT.Abs)
 
         def load_words(z):
-            table = keep.tile([P, T], I32, name=f"word_table{z}", align_bytes=64)
+            table = keep.tile([P, T], I32, name=f"word_table{z}", align_bytes=256)
             nc.sync.dma_start(out=table[:], in_=x_words[z].rearrange("p c r -> p (c r)").bitcast(I32))
             return table
 
         def load_rows(name, rows):
-            raw = keep.tile([P, PACK, rows.shape[1]], F32, name=name, align_bytes=64)
+            raw = keep.tile([P, PACK, rows.shape[1]], F32, name=name, align_bytes=256)
             nc.sync.dma_start(out=raw[:], in_=rows.rearrange("(p j) c -> p j c", j=PACK))
             return raw
 
@@ -60,7 +60,7 @@ def tile_picked_siam_abs_p_kernel(tc, x_words, x_scales, w1, w2, offs, out):
                 in_=x_scales[:, 4 * q : 4 * q + 4, :].bitcast(I32),
             )
         def load_row_pair(z, half):
-            raw = keep.tile([P, 2, H], F32, name=f"w1_raw{z}_{half}", align_bytes=64)
+            raw = keep.tile([P, 2, H], F32, name=f"w1_raw{z}_{half}", align_bytes=256)
             rows = w1[z * K_PASS : (z + 1) * K_PASS, :].rearrange("(p j) c -> p j c", j=PACK)
             nc.sync.dma_start(out=raw[:], in_=rows[:, 2 * half : 2 * half + 2, :])
             return raw
@@ -76,7 +76,7 @@ def tile_picked_siam_abs_p_kernel(tc, x_words, x_scales, w1, w2, offs, out):
             return slice(side * V + c * CHUNK, side * V + (c + 1) * CHUNK)
 
         def interleave(z, tag):
-            grouped = keep.tile([P, PACK * P * PACK], BF16, name=f"w1_grouped{z}", tag=tag, align_bytes=64)
+            grouped = keep.tile([P, PACK * P * PACK], BF16, name=f"w1_grouped{z}", tag=tag, align_bytes=256)
             rows = PACK // len(w1_raw[z])
             for i, raw in enumerate(w1_raw[z]):
                 src = raw[:].rearrange("p j (m t) -> p m j t", t=PACK)
@@ -87,8 +87,8 @@ def tile_picked_siam_abs_p_kernel(tc, x_words, x_scales, w1, w2, offs, out):
             return grouped
 
         def quantize(name, grouped, width):
-            code = keep.tile([P, width], U32, name=name + "_code", align_bytes=64)
-            scale = keep.tile([P, width], U8, name=name + "_scale", align_bytes=64)
+            code = keep.tile([P, width], U32, name=name + "_code", align_bytes=256)
+            scale = keep.tile([P, width], U8, name=name + "_scale", align_bytes=256)
             nc.vector.quantize_mx(out=code[:].bitcast(FP8X4), scales=scale[:], in_=grouped)
             return code, scale
 
@@ -109,8 +109,8 @@ def tile_picked_siam_abs_p_kernel(tc, x_words, x_scales, w1, w2, offs, out):
                 stop=(z == PASSES - 1 and t == PACK - 1),
             )
 
-        x_code0 = keep.tile([P, S], U32, name="x_code0", align_bytes=64)
-        x_scale = keep.tile([P, S], U8, name="x_scale", align_bytes=64)
+        x_code0 = keep.tile([P, S], U32, name="x_code0", align_bytes=256)
+        x_scale = keep.tile([P, S], U8, name="x_scale", align_bytes=256)
         nc.vector.tensor_copy(x_code0[:], word_table0[:].bitcast(U32).indirect(offsets[:]))
         nc.vector.tensor_copy(x_scale[:], scale_table[:].indirect(offsets[:]))
         grouped0 = interleave(0, "g0")
@@ -120,7 +120,7 @@ def tile_picked_siam_abs_p_kernel(tc, x_words, x_scales, w1, w2, offs, out):
                 product(0, key, t, coded, x_code0)
 
         grouped1 = interleave(1, "g1")
-        x_code1 = keep.tile([P, S], U32, name="x_code1", align_bytes=64)
+        x_code1 = keep.tile([P, S], U32, name="x_code1", align_bytes=256)
 
         def gather_last_pass(key):
             cols = entries(*key)
@@ -135,7 +135,7 @@ def tile_picked_siam_abs_p_kernel(tc, x_words, x_scales, w1, w2, offs, out):
             for t in range(PACK):
                 product(1, key, t, coded, x_code1)
 
-        w2_grouped = keep.tile([P, N, PACK], BF16, name="w2_grouped", align_bytes=64)
+        w2_grouped = keep.tile([P, N, PACK], BF16, name="w2_grouped", align_bytes=256)
         nc.scalar.copy(
             out=w2_grouped[:].rearrange("p (c i) j -> p c j i", i=4),
             in_=w2_raw[:].rearrange("p j (c i) -> p c j i", i=4),
@@ -145,8 +145,8 @@ def tile_picked_siam_abs_p_kernel(tc, x_words, x_scales, w1, w2, offs, out):
         def bank_view(side, lo, hi):
             return hidden[lo // CHUNK, side][:, :, lo % CHUNK : lo % CHUNK + hi - lo].rearrange("p t v -> p v t")
 
-        diff = keep.tile([P, V, PACK], BF16, name="diff", align_bytes=64)
-        second_relu = keep.tile([P, V, PACK], F32, name="second_relu", align_bytes=64)
+        diff = keep.tile([P, V, PACK], BF16, name="diff", align_bytes=256)
+        second_relu = keep.tile([P, V, PACK], F32, name="second_relu", align_bytes=256)
         for lo in range(0, V, PIECE):
             nc.scalar.activation(second_relu[:, lo : lo + PIECE, :], bank_view(SECOND, lo, lo + PIECE), ACT.Relu)
         for lo, hi in zip(CUTS, CUTS[1:]):
@@ -159,12 +159,12 @@ def tile_picked_siam_abs_p_kernel(tc, x_words, x_scales, w1, w2, offs, out):
                 op1=ALU.subtract,
             )
 
-        z_grouped = keep.tile([P, V * PACK], BF16, name="z_grouped", align_bytes=64)
+        z_grouped = keep.tile([P, V * PACK], BF16, name="z_grouped", align_bytes=256)
 
         def flat(lo, hi):
             return slice(lo * PACK, hi * PACK)
 
-        result = keep.tile([P, V], F32, name="result", align_bytes=64)
+        result = keep.tile([P, V], F32, name="result", align_bytes=256)
 
         def project(lo, hi, copy):
             z_code, z_scale = quantize(f"z{lo}", z_grouped[:, flat(lo, hi)], hi - lo)

@@ -196,8 +196,8 @@ def tile_picked_siam_abs_p_kernel(tc, x_words, x_scales, w1, w2, offs, out):
             op0=ALU.mult,
             op1=ALU.max,
         )
-        project(0, CHUNK, nc.scalar.copy)
-        project(CHUNK, V - PIECE, nc.scalar.copy)
-        nc.scalar.dma_start(out=out[:, : V - PIECE], in_=result[:, : V - PIECE])
-        project(V - PIECE, V, nc.vector.tensor_copy)
-        nc.sync.dma_start(out=out[:, V - PIECE :], in_=result[:, V - PIECE :])
+        project(0, CHUNK, nc.vector.tensor_copy)
+        project(CHUNK, V - PIECE, nc.vector.tensor_copy)
+        nc.sync.dma_start(out=out[:, : V - PIECE], in_=result[:, : V - PIECE])
+        project(V - PIECE, V, nc.scalar.copy)
+        nc.scalar.dma_start(out=out[:, V - PIECE :], in_=result[:, V - PIECE :])

@@ -24,7 +24,8 @@ CHUNK = 128
 CHUNKS = V // CHUNK
 PIECE = CHUNK // 2
 FIRST, SECOND = 0, 1
-VECTOR_ABS = slice(160, 192)
+VECTOR_ABS = ((160, 192), (192, 224))
+SCALAR_ABS = ((0, 64), (64, 128), (128, 160), (224, 256))
 CUTS = (0, 64, 128, 192, 224, 256)
 VECTOR_COLS = (96, 64)
 
@@ -183,19 +184,17 @@ def tile_picked_siam_abs_p_kernel(tc, x_words, x_scales, w1, w2, offs, out):
         def signed(lo, hi):
             return diff[:, lo:hi, :].rearrange("p v t -> p (v t)")
 
-        for lo, hi in zip(CUTS, CUTS[1:]):
-            hi = VECTOR_ABS.start if hi == VECTOR_ABS.stop else hi
-            if hi > lo:
-                nc.scalar.activation(z_grouped[:, flat(lo, hi)], signed(lo, hi), ACT.Abs)
-        lo, hi = VECTOR_ABS.start, VECTOR_ABS.stop
-        nc.vector.scalar_tensor_tensor(
-            out=z_grouped[:, flat(lo, hi)],
-            in0=signed(lo, hi),
-            scalar=-1.0,
-            in1=signed(lo, hi),
-            op0=ALU.mult,
-            op1=ALU.max,
-        )
+        for lo, hi in SCALAR_ABS:
+            nc.scalar.activation(z_grouped[:, flat(lo, hi)], signed(lo, hi), ACT.Abs)
+        for lo, hi in VECTOR_ABS:
+            nc.vector.scalar_tensor_tensor(
+                out=z_grouped[:, flat(lo, hi)],
+                in0=signed(lo, hi),
+                scalar=-1.0,
+                in1=signed(lo, hi),
+                op0=ALU.mult,
+                op1=ALU.max,
+            )
         project(0, CHUNK, nc.vector.tensor_copy)
         project(CHUNK, V - PIECE, nc.vector.tensor_copy)
         nc.sync.dma_start(out=out[:, : V - PIECE], in_=result[:, : V - PIECE])

@@ -195,8 +195,8 @@ def tile_picked_siam_abs_p_kernel(tc, x_words, x_scales, w1, w2, offs, out):
                 op0=ALU.mult,
                 op1=ALU.max,
             )
-        project(0, CHUNK, nc.vector.tensor_copy)
+        project(0, CHUNK, nc.scalar.copy)
+        nc.sync.dma_start(out=out[:, :CHUNK], in_=result[:, :CHUNK])
         project(CHUNK, V - PIECE, nc.vector.tensor_copy)
-        nc.sync.dma_start(out=out[:, : V - PIECE], in_=result[:, : V - PIECE])
         project(V - PIECE, V, nc.scalar.copy)
-        nc.scalar.dma_start(out=out[:, V - PIECE :], in_=result[:, V - PIECE :])
+        nc.scalar.dma_start(out=out[:, CHUNK:], in_=result[:, CHUNK:])

@@ -197,6 +197,6 @@ def tile_picked_siam_abs_p_kernel(tc, x_words, x_scales, w1, w2, offs, out):
             )
         project(0, CHUNK, nc.scalar.copy)
         nc.sync.dma_start(out=out[:, :CHUNK], in_=result[:, :CHUNK])
-        project(CHUNK, V - PIECE, nc.vector.tensor_copy)
+        project(CHUNK, V - PIECE, nc.scalar.copy)
         project(V - PIECE, V, nc.scalar.copy)
         nc.scalar.dma_start(out=out[:, CHUNK:], in_=result[:, CHUNK:])

@@ -28,6 +28,7 @@ VECTOR_ABS = ((160, 192), (192, 224))
 SCALAR_ABS = ((0, 64), (64, 128), (128, 160), (224, 256))
 CUTS = (0, 64, 128, 192, 224, 256)
 VECTOR_COLS = (96, 64)
+HALF_COLS = (44, 36)
 
 
 def tile_picked_siam_abs_p_kernel(tc, x_words, x_scales, w1, w2, offs, out):
@@ -60,13 +61,9 @@ def tile_picked_siam_abs_p_kernel(tc, x_words, x_scales, w1, w2, offs, out):
                 out=scale_table[32 * q : 32 * q + 4 * PASSES, :].bitcast(I32),
                 in_=x_scales[:, 4 * q : 4 * q + 4, :].bitcast(I32),
             )
-        def load_row_pair(z, half):
-            raw = keep.tile([P, 2, H], F32, name=f"w1_raw{z}_{half}", align_bytes=256)
-            rows = w1[z * K_PASS : (z + 1) * K_PASS, :].rearrange("(p j) c -> p j c", j=PACK)
-            nc.sync.dma_start(out=raw[:], in_=rows[:, 2 * half : 2 * half + 2, :])
-            return raw
 
-        w1_raw = [[load_rows("w1_raw0", w1[:K_PASS, :])], [load_row_pair(1, half) for half in range(2)]]
+        w1_first = load_rows("w1_raw0", w1[:K_PASS, :])
+        w1_last = [load_rows(f"w1_raw1_{h}", w1[K_PASS:, h * H // 2 : (h + 1) * H // 2]) for h in range(2)]
         word_table1 = load_words(1)
         w2_raw = load_rows("w2_raw", w2)
 
@@ -76,16 +73,12 @@ def tile_picked_siam_abs_p_kernel(tc, x_words, x_scales, w1, w2, offs, out):
         def entries(c, side):
             return slice(side * V + c * CHUNK, side * V + (c + 1) * CHUNK)
 
-        def interleave(z, tag):
-            grouped = keep.tile([P, PACK * P * PACK], BF16, name=f"w1_grouped{z}", tag=tag, align_bytes=256)
-            rows = PACK // len(w1_raw[z])
-            for i, raw in enumerate(w1_raw[z]):
-                src = raw[:].rearrange("p j (m t) -> p m j t", t=PACK)
-                dst = grouped[:].rearrange("p (t m j) -> p m j t", t=PACK, j=PACK)[:, :, i * rows : (i + 1) * rows, :]
-                for tiles, cols in zip((slice(0, 2), slice(2, 4)), VECTOR_COLS):
-                    nc.vector.tensor_copy(out=dst[:, :cols, :, tiles], in_=src[:, :cols, :, tiles])
-                    nc.scalar.copy(out=dst[:, cols:, :, tiles], in_=src[:, cols:, :, tiles])
-            return grouped
+        def interleave(grouped, raw, first, shares):
+            src = raw[:].rearrange("p j (m t) -> p m j t", t=PACK)
+            dst = grouped[:].rearrange("p (t m j) -> p m j t", t=PACK, j=PACK)[:, first : first + src.shape[1]]
+            for tiles, cols in zip((slice(0, 2), slice(2, 4)), shares):
+                nc.vector.tensor_copy(out=dst[:, :cols, :, tiles], in_=src[:, :cols, :, tiles])
+                nc.scalar.copy(out=dst[:, cols:, :, tiles], in_=src[:, cols:, :, tiles])
 
         def quantize(name, grouped, width):
             code = keep.tile([P, width], U32, name=name + "_code", align_bytes=256)
@@ -114,13 +107,25 @@ def tile_picked_siam_abs_p_kernel(tc, x_words, x_scales, w1, w2, offs, out):
         x_scale = keep.tile([P, S], U8, name="x_scale", align_bytes=256)
         nc.vector.tensor_copy(x_code0[:], word_table0[:].bitcast(U32).indirect(offsets[:]))
         nc.vector.tensor_copy(x_scale[:], scale_table[:].indirect(offsets[:]))
-        grouped0 = interleave(0, "g0")
+        grouped0 = keep.tile([P, PACK * P * PACK], BF16, name="w1_grouped0", align_bytes=256)
+        interleave(grouped0, w1_first, 0, VECTOR_COLS)
         coded = quantize_tiles(0, grouped0, 0, 2) + quantize_tiles(0, grouped0, 2, 4)
         for t in range(PACK):
             for key in banks:
                 product(0, key, t, coded, x_code0)
 
-        grouped1 = interleave(1, "g1")
+        grouped1 = keep.tile([P, PACK * P * PACK], BF16, name="w1_grouped1", align_bytes=256)
+        last_code = keep.tile([P, H], U32, name="last_code", align_bytes=256)
+        last_scale = keep.tile([P, H], U8, name="last_scale", align_bytes=256)
+        for h in range(2):
+            interleave(grouped1, w1_last[h], h * P // 2, HALF_COLS)
+            for t in range(PACK):
+                lo = t * P + h * P // 2
+                nc.vector.quantize_mx(
+                    out=last_code[:, lo : lo + P // 2].bitcast(FP8X4),
+                    scales=last_scale[:, lo : lo + P // 2],
+                    in_=grouped1[:, lo * PACK : (lo + P // 2) * PACK],
+                )
         x_code1 = keep.tile([P, S], U32, name="x_code1", align_bytes=256)
 
         def gather_last_pass(key):
@@ -129,7 +134,7 @@ def tile_picked_siam_abs_p_kernel(tc, x_words, x_scales, w1, w2, offs, out):
                 x_code1[:, cols], word_table1[:].bitcast(U32).indirect(offsets[:, cols.start // 16 : cols.stop // 16])
             )
 
-        coded = quantize_tiles(1, grouped1, 0, 2) + quantize_tiles(1, grouped1, 2, 4)
+        coded = [(last_code[:, t * P : (t + 1) * P], last_scale[:, t * P : (t + 1) * P]) for t in range(PACK)]
         for key in banks:
             gather_last_pass(key)
         for key in banks:

from contextlib import ExitStack

import concourse.mybir as mybir

K, T, S, V, H, N = 1024, 1024, 512, 256, 512, 128
FLOPS = 2 * K * H * S + 2 * H * N * V

F32 = mybir.dt.float32
BF16 = mybir.dt.bfloat16
I32 = mybir.dt.int32
U32 = mybir.dt.uint32
U16 = mybir.dt.uint16
U8 = mybir.dt.uint8
FP8X4 = mybir.dt.float8_e4m3fn_x4
ALU = mybir.AluOpType
ACT = mybir.ActivationFunctionType

P = 128
PACK = 4
K_PASS = P * PACK
PASSES = K // K_PASS
QUADS = 4
CHUNK = 128
CHUNKS = V // CHUNK
PIECE = CHUNK // 2
FIRST, SECOND = 0, 1
VECTOR_ABS = ((160, 192), (192, 224))
SCALAR_ABS = ((0, 64), (64, 128), (128, 160), (224, 256))
CUTS = (0, 64, 128, 192, 224, 256)
VECTOR_COLS = (96, 64)
HALF_COLS = (44, 36)


def tile_picked_siam_abs_p_kernel(tc, x_words, x_scales, w1, w2, offs, out):
    nc = tc.nc
    with ExitStack() as ctx:
        keep = ctx.enter_context(tc.tile_pool(name="keep", bufs=1))
        psum = ctx.enter_context(tc.psum_pool(name="psum", bufs=1))

        offsets = keep.tile([P, S // 16], U16, name="offsets")
        scale_table = keep.tile([P, T], U8, name="scale_table", align_bytes=256)
        nc.vector.memset(scale_table[:].bitcast(I32), 0)
        warm = keep.tile([P, 16], F32, name="warm", align_bytes=256)
        nc.gpsimd.memset(warm[:, 0:1], 0.0)
        nc.scalar.activation(warm[:, 8:9], warm[:, 0:1], ACT.Abs)

        def load_words(z):
            table = keep.tile([P, T], I32, name=f"word_table{z}", align_bytes=256)
            nc.sync.dma_start(out=table[:], in_=x_words[z].rearrange("p c r -> p (c r)").bitcast(I32))
            return table

        def load_rows(name, rows):
            raw = keep.tile([P, PACK, rows.shape[1]], F32, name=name, align_bytes=256)
            nc.sync.dma_start(out=raw[:], in_=rows.rearrange("(p j) c -> p j c", j=PACK))
            return raw

        word_table0 = load_words(0)
        nc.sync.dma_start(offsets[:], offs)
        for q in range(QUADS):
            nc.sync.dma_start(
                out=scale_table[32 * q : 32 * q + 4 * PASSES, :].bitcast(I32),
                in_=x_scales[:, 4 * q : 4 * q + 4, :].bitcast(I32),
            )

        w1_first = load_rows("w1_raw0", w1[:K_PASS, :])
        w1_last = [load_rows(f"w1_raw1_{h}", w1[K_PASS:, h * H // 2 : (h + 1) * H // 2]) for h in range(2)]
        word_table1 = load_words(1)
        w2_raw = load_rows("w2_raw", w2)

        banks = [(c, side) for c in range(CHUNKS) for side in (SECOND, FIRST)]
        hidden = {key: psum.tile([P, PACK, CHUNK], F32, name=f"hidden{key[0]}_{key[1]}") for key in banks}

        def entries(c, side):
            return slice(side * V + c * CHUNK, side * V + (c + 1) * CHUNK)

        def interleave(grouped, raw, first, shares):
            src = raw[:].rearrange("p j (m t) -> p m j t", t=PACK)
            dst = grouped[:].rearrange("p (t m j) -> p m j t", t=PACK, j=PACK)[:, first : first + src.shape[1]]
            for tiles, cols in zip((slice(0, 2), slice(2, 4)), shares):
                nc.vector.tensor_copy(out=dst[:, :cols, :, tiles], in_=src[:, :cols, :, tiles])
                nc.scalar.copy(out=dst[:, cols:, :, tiles], in_=src[:, cols:, :, tiles])

        def quantize(name, grouped, width):
            code = keep.tile([P, width], U32, name=name + "_code", align_bytes=256)
            scale = keep.tile([P, width], U8, name=name + "_scale", align_bytes=256)
            nc.vector.quantize_mx(out=code[:].bitcast(FP8X4), scales=scale[:], in_=grouped)
            return code, scale

        def quantize_tiles(z, grouped, lo, hi):
            code, scale = quantize(f"w1_{z}_{lo}", grouped[:, lo * K_PASS : hi * K_PASS], (hi - lo) * P)
            return [(code[:, s * P : (s + 1) * P], scale[:, s * P : (s + 1) * P]) for s in range(hi - lo)]

        def product(z, key, t, coded, x_code):
            code, scale = coded[t]
            cols = entries(*key)
            nc.tensor.matmul_mx(
                out=hidden[key][:, t, :],
                lhsT=code.bitcast(FP8X4),
                lhsT_scale=scale,
                rhs=x_code[:, cols].bitcast(FP8X4),
                rhs_scale=x_scale[4 * z : P, cols],
                start=(z == 0 and t == 0),
                stop=(z == PASSES - 1 and t == PACK - 1),
            )

        x_code0 = keep.tile([P, S], U32, name="x_code0", align_bytes=256)
        x_scale = keep.tile([P, S], U8, name="x_scale", align_bytes=256)
        nc.vector.tensor_copy(x_code0[:], word_table0[:].bitcast(U32).indirect(offsets[:]))
        nc.vector.tensor_copy(x_scale[:], scale_table[:].indirect(offsets[:]))
        grouped0 = keep.tile([P, PACK * P * PACK], BF16, name="w1_grouped0", align_bytes=256)
        interleave(grouped0, w1_first, 0, VECTOR_COLS)
        coded = quantize_tiles(0, grouped0, 0, 2) + quantize_tiles(0, grouped0, 2, 4)
        for t in range(PACK):
            for key in banks:
                product(0, key, t, coded, x_code0)

        grouped1 = keep.tile([P, PACK * P * PACK], BF16, name="w1_grouped1", align_bytes=256)
        last_code = keep.tile([P, H], U32, name="last_code", align_bytes=256)
        last_scale = keep.tile([P, H], U8, name="last_scale", align_bytes=256)
        for h in range(2):
            interleave(grouped1, w1_last[h], h * P // 2, HALF_COLS)
            for t in range(PACK):
                lo = t * P + h * P // 2
                nc.vector.quantize_mx(
                    out=last_code[:, lo : lo + P // 2].bitcast(FP8X4),
                    scales=last_scale[:, lo : lo + P // 2],
                    in_=grouped1[:, lo * PACK : (lo + P // 2) * PACK],
                )
        x_code1 = keep.tile([P, S], U32, name="x_code1", align_bytes=256)

        def gather_last_pass(key):
            cols = entries(*key)
            nc.vector.tensor_copy(
                x_code1[:, cols], word_table1[:].bitcast(U32).indirect(offsets[:, cols.start // 16 : cols.stop // 16])
            )

        coded = [(last_code[:, t * P : (t + 1) * P], last_scale[:, t * P : (t + 1) * P]) for t in range(PACK)]
        for key in banks:
            gather_last_pass(key)
        for key in banks:
            for t in range(PACK):
                product(1, key, t, coded, x_code1)

        w2_grouped = keep.tile([P, N, PACK], BF16, name="w2_grouped", align_bytes=256)
        nc.scalar.copy(
            out=w2_grouped[:].rearrange("p (c i) j -> p c j i", i=4),
            in_=w2_raw[:].rearrange("p j (c i) -> p c j i", i=4),
        )
        w2_code, w2_scale = quantize("w2", w2_grouped[:].rearrange("p c j -> p (c j)"), N)

        def bank_view(side, lo, hi):
            return hidden[lo // CHUNK, side][:, :, lo % CHUNK : lo % CHUNK + hi - lo].rearrange("p t v -> p v t")

        diff = keep.tile([P, V, PACK], BF16, name="diff", align_bytes=256)
        second_relu = keep.tile([P, V, PACK], F32, name="second_relu", align_bytes=256)
        for lo in range(0, V, PIECE):
            nc.scalar.activation(second_relu[:, lo : lo + PIECE, :], bank_view(SECOND, lo, lo + PIECE), ACT.Relu)
        for lo, hi in zip(CUTS, CUTS[1:]):
            nc.vector.scalar_tensor_tensor(
                out=diff[:, lo:hi, :],
                in0=bank_view(FIRST, lo, hi),
                scalar=0.0,
                in1=second_relu[:, lo:hi, :],
                op0=ALU.max,
                op1=ALU.subtract,
            )

        z_grouped = keep.tile([P, V * PACK], BF16, name="z_grouped", align_bytes=256)

        def flat(lo, hi):
            return slice(lo * PACK, hi * PACK)

        result = keep.tile([P, V], F32, name="result", align_bytes=256)

        def project(lo, hi, copy):
            z_code, z_scale = quantize(f"z{lo}", z_grouped[:, flat(lo, hi)], hi - lo)
            projected = psum.tile([P, hi - lo], F32, name=f"projected{lo}")
            nc.tensor.matmul_mx(
                out=projected[:],
                lhsT=w2_code[:].bitcast(FP8X4),
                lhsT_scale=w2_scale[:],
                rhs=z_code[:].bitcast(FP8X4),
                rhs_scale=z_scale[:],
                start=True,
                stop=True,
            )
            copy(out=result[:, lo:hi], in_=projected[:])

        def signed(lo, hi):
            return diff[:, lo:hi, :].rearrange("p v t -> p (v t)")

        for lo, hi in SCALAR_ABS:
            nc.scalar.activation(z_grouped[:, flat(lo, hi)], signed(lo, hi), ACT.Abs)
        for lo, hi in VECTOR_ABS:
            nc.vector.scalar_tensor_tensor(
                out=z_grouped[:, flat(lo, hi)],
                in0=signed(lo, hi),
                scalar=-1.0,
                in1=signed(lo, hi),
                op0=ALU.mult,
                op1=ALU.max,
            )
        project(0, CHUNK, nc.scalar.copy)
        nc.sync.dma_start(out=out[:, :CHUNK], in_=result[:, :CHUNK])
        project(CHUNK, V - PIECE, nc.scalar.copy)
        project(V - PIECE, V, nc.scalar.copy)
        nc.scalar.dma_start(out=out[:, CHUNK:], in_=result[:, CHUNK:])
